import numpy as np
import ml_dtypes


def mxq(x, axis, fmt="e4m3"):
    dtype, down = {"e4m3": (ml_dtypes.float8_e4m3fn, 7), "e5m2": (ml_dtypes.float8_e5m2, 14)}[fmt]
    v = np.moveaxis(np.asarray(x, np.float32).astype(ml_dtypes.bfloat16).astype(np.float64), axis, -1)
    blocks = v.reshape(v.shape[:-1] + (-1, 32))
    amax = np.abs(blocks).max(-1, keepdims=True)
    byte = np.maximum(np.where(amax > 0, np.frexp(amax)[1] - 1 + 127, 0) - down, 1)
    scale = np.exp2(byte - 127.0)
    codes = (blocks / scale).astype(np.float32).astype(dtype).astype(np.float64)
    return np.moveaxis((codes * scale).reshape(v.shape), -1, axis)


WIDE = False


def mx_kscale(k):
    if not WIDE:
        return np.ones(k)
    levels = np.array([10, -10, 5, -5, 0])
    if k % 512:
        return np.exp2(np.random.permutation(np.resize(levels, k // 32))).repeat(32)
    a = np.empty((k // 512, 16))
    for p in range(k // 512):
        a[p, :8] = np.random.permutation(np.resize(levels, 8))
        for g in range(8):
            far = levels[np.abs(levels - a[p, g]) >= 10]
            a[p, g + 8] = far[np.random.randint(len(far))]
    return np.exp2(a.ravel()).repeat(32)


def f64(x):
    return np.asarray(x).astype(np.float64)


def striped(idx):
    return np.tile(idx.reshape(-1, 16).T, (8, 1)).astype(np.uint16)


def unstriped(offs):
    return offs[:16].T.reshape(-1).astype(np.int64)


K, T, E, C, N = 1024, 640, 4, 128, 384


def by_expert(wq, xq):
    return np.concatenate([wq[e].T @ xq[:, e * C:(e + 1) * C] for e in range(E)], axis=1)


def setup_inputs():
    n = np.random.standard_normal
    s = mx_kscale(K)[:, None]
    return {
        "xT": (n((K, T)) * s).astype(np.float32),
        "w": (n((E, K, N)) / np.sqrt(K) / s[None]).astype(np.float32),
        "b": (0.3 * n((N, E))).astype(np.float32),
        "gate": np.tile(np.random.uniform(0.2, 1.0, E * C), (N, 1)).astype(np.float32),
        "offs": striped(np.random.permutation(T)[:E * C]),
        "dst": striped(np.random.permutation(T)[:E * C]),
    }


def reference(xT, w, b, gate, offs, dst):
    idx = unstriped(offs)
    xq = mxq(f64(xT)[:, idx], 0, "e4m3")
    y = by_expert(mxq(f64(w), 1, "e4m3"), xq)
    y = y + np.repeat(f64(b), C, axis=1)
    out = np.zeros((N, T))
    out[:, unstriped(dst)] = f64(gate) * y
    return out

@@ -1,0 +1,178 @@
+from contextlib import ExitStack
+
+import concourse.mybir as mybir
+
+K, T, E, C, N = 1024, 640, 4, 128, 384
+FLOPS = 2 * K * N * E * C
+
+F32 = mybir.dt.float32
+BF16 = mybir.dt.bfloat16
+U32 = mybir.dt.uint32
+U16 = mybir.dt.uint16
+U8 = mybir.dt.uint8
+FP8X4 = mybir.dt.float8_e4m3fn_x4
+COPY = mybir.ActivationFunctionType.Copy
+IDENTITY = mybir.ActivationFunctionType.Identity
+MULT = mybir.AluOpType.mult
+ADD = mybir.AluOpType.add
+
+P = 128
+PACK = 4
+K_PASS = P * PACK
+PASSES = K // K_PASS
+N_TILES = N // P
+SLOTS = E * C
+
+
+def interleave(nc, engine, grouped, raw):
+    dst = grouped.rearrange("p (c i) j -> p c j i", i=4)
+    src = raw.rearrange("p j (c i) -> p c j i", i=4)
+    if engine == "vector":
+        nc.vector.tensor_copy(out=dst, in_=src)
+    else:
+        nc.scalar.activation(dst, src, COPY)
+
+
+def quantize(nc, codes, scales, grouped):
+    nc.vector.quantize_mx(
+        out=codes.bitcast(FP8X4),
+        scales=scales,
+        in_=grouped.rearrange("p w j -> p (w j)"),
+    )
+
+
+def tile_moe_two_lin_bias_kernel(tc, xT, w, b, gate, offs, dst, out):
+    nc = tc.nc
+    with ExitStack() as ctx:
+        keep = ctx.enter_context(tc.tile_pool(name="keep", bufs=1))
+        psum = ctx.enter_context(tc.psum_pool(name="psum", bufs=8))
+
+        offs_sb = keep.tile([P, SLOTS // 16], U16, name="offs_sb")
+        dst_sb = keep.tile([P, SLOTS // 16], U16, name="dst_sb")
+        b_sb = keep.tile([P, N_TILES, 8], F32, name="b_sb")
+        gate_sb = keep.tile([P, N_TILES, SLOTS], F32, name="gate_sb")
+        warm = keep.tile([P, 8], F32, name="warm")
+        windows = [keep.tile([P, T], F32, name=f"window{n}") for n in range(N_TILES)]
+        x_scales = keep.tile([P, T], U8, name="x_scales", align_bytes=64)
+        slot_scales = keep.tile([P, SLOTS], U8, name="slot_scales", align_bytes=64)
+        x_codes = [keep.tile([P, T], U32, name=f"x_codes{a}", align_bytes=64) for a in range(PASSES)]
+        slot_codes = [keep.tile([P, SLOTS], U32, name=f"slot_codes{a}", align_bytes=64) for a in range(PASSES)]
+
+        nc.vector.memset(warm[:], 0.0)
+        nc.scalar.activation(warm[:, 1:2], warm[:, 0:1], IDENTITY)
+        nc.gpsimd.memset(x_scales[:], 0)
+        for window in windows:
+            nc.vector.memset(window[:], 0.0)
+
+        nc.scalar.dma_start(out=b_sb[:, :, 0:E], in_=b.rearrange("(t p) e -> p t e", p=P))
+        x_cuts = [(0, 256), (256, 640)]
+        x_raw = {}
+        for a in range(PASSES):
+            rows = xT[a * K_PASS:(a + 1) * K_PASS, :].rearrange("(p j) t -> p j t", j=PACK)
+            for lo, hi in x_cuts:
+                x_raw[a, lo] = keep.tile([P, PACK, hi - lo], F32, name=f"x_raw{a}_{lo}")
+                nc.sync.dma_start(out=x_raw[a, lo][:], in_=rows[:, :, lo:hi])
+            if a == 0:
+                nc.sync.dma_start(offs_sb[:], offs)
+        nc.sync.dma_start(dst_sb[:], dst)
+
+        w_raw = {}
+
+        def load_w(e, a, lo, hi):
+            rows = w[e, a * K_PASS:(a + 1) * K_PASS, :].rearrange("(p j) n -> p j n", j=PACK)
+            w_raw[e, a, lo] = keep.tile([P, PACK, hi - lo], F32, name=f"w_raw{e}_{a}_{lo}")
+            nc.sync.dma_start(out=w_raw[e, a, lo][:], in_=rows[:, :, lo:hi])
+
+        for e in range(E):
+            if e < E - 1:
+                for a in range(PASSES):
+                    load_w(e, a, 0, N)
+            else:
+                for lo, hi in ((0, 256), (256, N)):
+                    for a in range(PASSES):
+                        load_w(e, a, lo, hi)
+            if e == 0:
+                nc.sync.dma_start(out=gate_sb[:], in_=gate.rearrange("(t p) s -> p t s", p=P))
+
+        def take_x(a, lo, hi, engine):
+            src = 0 if lo < 256 else 256
+            grouped = keep.tile([P, hi - lo, PACK], BF16, name=f"x_grouped{a}_{lo}", align_bytes=64)
+            interleave(nc, engine, grouped[:], x_raw[a, src][:, :, lo - src:hi - src])
+            return grouped
+
+        X_ENGINE = {(0, 0): "vector", (0, 256): "scalar", (0, 512): "vector",
+                    (1, 0): "scalar", (1, 256): "vector", (1, 512): "scalar"}
+        for a in range(PASSES):
+            groups = [(lo, hi, take_x(a, lo, hi, X_ENGINE[a, lo])) for lo, hi in ((0, 256), (256, 512), (512, 640))]
+            for lo, hi, grouped in groups:
+                quantize(nc, x_codes[a][:, lo:hi], x_scales[4 * a:P, lo:hi], grouped[:])
+            if a == 0:
+                for h in range(2):
+                    nc.vector.tensor_copy(
+                        out=slot_codes[a][:, h * 256:(h + 1) * 256],
+                        in_=x_codes[a][:].indirect(offs_sb[:, h * 16:(h + 1) * 16]))
+        for h in range(2):
+            nc.vector.tensor_copy(
+                out=slot_codes[1][:, h * 256:(h + 1) * 256],
+                in_=x_codes[1][:].indirect(offs_sb[:, h * 16:(h + 1) * 16]))
+            nc.vector.tensor_copy(
+                out=slot_scales[:, h * 256:(h + 1) * 256],
+                in_=x_scales[:].indirect(offs_sb[:, h * 16:(h + 1) * 16]))
+
+        def take_w(e, a, lo, hi, engine):
+            src = lo if (e, a, lo) in w_raw else (256 if (e, a, 256) in w_raw and lo >= 256 else 0)
+            grouped = keep.tile([P, hi - lo, PACK], BF16, name=f"w_grouped{e}_{a}_{lo}", align_bytes=64)
+            interleave(nc, engine, grouped[:], w_raw[e, a, src][:, :, lo - src:hi - src])
+            return grouped
+
+        W_ENGINE = {(0, 0, 0): "scalar", (0, 0, 256): "vector", (0, 1, 0): "scalar", (0, 1, 256): "vector",
+                    (3, 0, 256): "vector"}
+        products = {}
+        w_codes, w_scales = {}, {}
+        for e in range(E):
+            for a in range(PASSES):
+                w_codes[e, a] = keep.tile([P, N], U32, name=f"w_codes{e}_{a}", align_bytes=64)
+                w_scales[e, a] = keep.tile([P, N], U8, name=f"w_scales{e}_{a}", align_bytes=64)
+
+        def multiply(e, n, acc):
+            cols = slice(n * P, (n + 1) * P)
+            slots = slice(e * C, (e + 1) * C)
+            for a in range(PASSES):
+                nc.tensor.matmul_mx(
+                    out=acc[:],
+                    lhsT=w_codes[e, a][:, cols].bitcast(FP8X4),
+                    lhsT_scale=w_scales[e, a][:, cols],
+                    rhs=slot_codes[a][:, slots].bitcast(FP8X4),
+                    rhs_scale=slot_scales[4 * a:P, slots],
+                    start=(a == 0), stop=(a == PASSES - 1))
+
+        def finish(e, n, acc):
+            y = keep.tile([P, C], F32, name=f"y{e}_{n}")
+            nc.scalar.activation(y[:], acc[:], IDENTITY, bias=b_sb[:, n, e:e + 1])
+            products[e, n] = y
+
+        def scatter(e, n):
+            nc.vector.tensor_tensor(
+                windows[n][:].indirect(dst_sb[:, e * 8:(e + 1) * 8]),
+                products[e, n][:], gate_sb[:, n, e * C:(e + 1) * C], MULT)
+
+        for e in range(E):
+            order = [(0, 0, 256), (0, 256, N), (1, 0, 256), (1, 256, N)]
+            if e == E - 1:
+                order = [(0, 0, 256), (1, 0, 256), (0, 256, N), (1, 256, N)]
+            for a, lo, hi in order:
+                grouped = take_w(e, a, lo, hi, W_ENGINE.get((e, a, lo), "scalar"))
+                quantize(nc, w_codes[e, a][:, lo:hi], w_scales[e, a][:, lo:hi], grouped[:])
+            accs = []
+            for n in range(N_TILES):
+                acc = psum.tile([P, C], F32, name="acc")
+                multiply(e, n, acc)
+                accs.append(acc)
+            for n in range(N_TILES):
+                finish(e, n, accs[n])
+            if e > 0:
+                for n in range(N_TILES):
+                    scatter(e - 1, n)
+        for n in range(N_TILES):
+            scatter(E - 1, n)
+            nc.sync.dma_start(out=out[n * P:(n + 1) * P, :], in_=windows[n][:])

@@ -148,13 +148,13 @@ def tile_moe_two_lin_bias_kernel(tc, xT, w, b, gate, offs, dst, out):
 
         def finish(e, n, acc):
             y = keep.tile([P, C], F32, name=f"y{e}_{n}")
-            nc.scalar.activation(y[:], acc[:], IDENTITY, bias=b_sb[:, n, e:e + 1])
+            nc.vector.scalar_tensor_tensor(y[:], acc[:], b_sb[:, n, e:e + 1], gate_sb[:, n, e * C:(e + 1) * C], ADD, MULT)
             products[e, n] = y
 
         def scatter(e, n):
-            nc.vector.tensor_tensor(
-                windows[n][:].indirect(dst_sb[:, e * 8:(e + 1) * 8]),
-                products[e, n][:], gate_sb[:, n, e * C:(e + 1) * C], MULT)
+            nc.vector.tensor_copy(
+                out=windows[n][:].indirect(dst_sb[:, e * 8:(e + 1) * 8]),
+                in_=products[e, n][:])
 
         for e in range(E):
             order = [(0, 0, 256), (0, 256, N), (1, 0, 256), (1, 256, N)]

@@ -22,6 +22,7 @@ K_PASS = P * PACK
 PASSES = K // K_PASS
 N_TILES = N // P
 SLOTS = E * C
+HALF = SLOTS // 2
 
 
 def interleave(nc, engine, grouped, raw):
@@ -29,6 +30,8 @@ def interleave(nc, engine, grouped, raw):
     src = raw.rearrange("p j (c i) -> p c j i", i=4)
     if engine == "vector":
         nc.vector.tensor_copy(out=dst, in_=src)
+    elif engine == "gpsimd":
+        nc.gpsimd.tensor_scalar(dst, src, 1.0, 0.0, MULT, ADD)
     else:
         nc.scalar.activation(dst, src, COPY)
 
@@ -57,6 +60,10 @@ def tile_moe_two_lin_bias_kernel(tc, xT, w, b, gate, offs, dst, out):
         slot_scales = keep.tile([P, SLOTS], U8, name="slot_scales", align_bytes=64)
         x_codes = [keep.tile([P, T], U32, name=f"x_codes{a}", align_bytes=64) for a in range(PASSES)]
         slot_codes = [keep.tile([P, SLOTS], U32, name=f"slot_codes{a}", align_bytes=64) for a in range(PASSES)]
+        x_raw = [keep.tile([P, PACK, T], F32, name=f"x_raw{a}") for a in range(PASSES)]
+        w_raw = {(e, a): keep.tile([P, PACK, N], F32, name=f"w_raw{e}_{a}") for e in range(E) for a in range(PASSES)}
+        w_codes = {(e, a): keep.tile([P, N], U32, name=f"w_codes{e}_{a}", align_bytes=64) for e in range(E) for a in range(PASSES)}
+        w_scales = {(e, a): keep.tile([P, N], U8, name=f"w_scales{e}_{a}", align_bytes=64) for e in range(E) for a in range(PASSES)}
 
         nc.vector.memset(warm[:], 0.0)
         nc.scalar.activation(warm[:, 1:2], warm[:, 0:1], IDENTITY)
@@ -65,114 +72,87 @@ def tile_moe_two_lin_bias_kernel(tc, xT, w, b, gate, offs, dst, out):
             nc.vector.memset(window[:], 0.0)
 
         nc.scalar.dma_start(out=b_sb[:, :, 0:E], in_=b.rearrange("(t p) e -> p t e", p=P))
-        x_cuts = [(0, 256), (256, 640)]
-        x_raw = {}
-        for a in range(PASSES):
-            rows = xT[a * K_PASS:(a + 1) * K_PASS, :].rearrange("(p j) t -> p j t", j=PACK)
-            for lo, hi in x_cuts:
-                x_raw[a, lo] = keep.tile([P, PACK, hi - lo], F32, name=f"x_raw{a}_{lo}")
-                nc.sync.dma_start(out=x_raw[a, lo][:], in_=rows[:, :, lo:hi])
-            if a == 0:
-                nc.sync.dma_start(offs_sb[:], offs)
+
+        def load_x(a):
+            nc.sync.dma_start(out=x_raw[a][:], in_=xT[a * K_PASS:(a + 1) * K_PASS, :].rearrange("(p j) t -> p j t", j=PACK))
+
+        def load_w(e, a):
+            nc.sync.dma_start(out=w_raw[e, a][:], in_=w[e, a * K_PASS:(a + 1) * K_PASS, :].rearrange("(p j) n -> p j n", j=PACK))
+
+        load_x(0)
+        nc.sync.dma_start(offs_sb[:], offs)
+        load_x(1)
         nc.sync.dma_start(dst_sb[:], dst)
+        load_w(0, 0)
+        load_w(0, 1)
+        nc.sync.dma_start(out=gate_sb[:], in_=gate.rearrange("(t p) s -> p t s", p=P))
+        for e in range(1, E):
+            for a in range(PASSES):
+                load_w(e, a)
 
-        w_raw = {}
+        X_ENGINES = (("scalar", "vector", "vector"), ("scalar", "vector", "scalar"))
 
-        def load_w(e, a, lo, hi):
-            rows = w[e, a * K_PASS:(a + 1) * K_PASS, :].rearrange("(p j) n -> p j n", j=PACK)
-            w_raw[e, a, lo] = keep.tile([P, PACK, hi - lo], F32, name=f"w_raw{e}_{a}_{lo}")
-            nc.sync.dma_start(out=w_raw[e, a, lo][:], in_=rows[:, :, lo:hi])
-
-        for e in range(E):
-            if e < E - 1:
-                for a in range(PASSES):
-                    load_w(e, a, 0, N)
-            else:
-                for lo, hi in ((0, 256), (256, N)):
-                    for a in range(PASSES):
-                        load_w(e, a, lo, hi)
-            if e == 0:
-                nc.sync.dma_start(out=gate_sb[:], in_=gate.rearrange("(t p) s -> p t s", p=P))
-
-        def take_x(a, lo, hi, engine):
-            src = 0 if lo < 256 else 256
-            grouped = keep.tile([P, hi - lo, PACK], BF16, name=f"x_grouped{a}_{lo}", align_bytes=64)
-            interleave(nc, engine, grouped[:], x_raw[a, src][:, :, lo - src:hi - src])
-            return grouped
-
-        X_ENGINE = {(0, 0): "vector", (0, 256): "scalar", (0, 512): "vector",
-                    (1, 0): "scalar", (1, 256): "vector", (1, 512): "scalar"}
-        for a in range(PASSES):
-            groups = [(lo, hi, take_x(a, lo, hi, X_ENGINE[a, lo])) for lo, hi in ((0, 256), (256, 512), (512, 640))]
-            for lo, hi, grouped in groups:
+        def take_x(a):
+            pieces = []
+            for (lo, hi), engine in zip(((0, 256), (256, 512), (512, 640)), X_ENGINES[a]):
+                grouped = keep.tile([P, hi - lo, PACK], BF16, name=f"x_grouped{a}_{lo}", align_bytes=64)
+                interleave(nc, engine, grouped[:], x_raw[a][:, :, lo:hi])
+                pieces.append((lo, hi, grouped))
+            for lo, hi, grouped in pieces:
                 quantize(nc, x_codes[a][:, lo:hi], x_scales[4 * a:P, lo:hi], grouped[:])
-            if a == 0:
-                for h in range(2):
-                    nc.vector.tensor_copy(
-                        out=slot_codes[a][:, h * 256:(h + 1) * 256],
-                        in_=x_codes[a][:].indirect(offs_sb[:, h * 16:(h + 1) * 16]))
-        for h in range(2):
-            nc.vector.tensor_copy(
-                out=slot_codes[1][:, h * 256:(h + 1) * 256],
-                in_=x_codes[1][:].indirect(offs_sb[:, h * 16:(h + 1) * 16]))
-            nc.vector.tensor_copy(
-                out=slot_scales[:, h * 256:(h + 1) * 256],
-                in_=x_scales[:].indirect(offs_sb[:, h * 16:(h + 1) * 16]))
 
-        def take_w(e, a, lo, hi, engine):
-            src = lo if (e, a, lo) in w_raw else (256 if (e, a, 256) in w_raw and lo >= 256 else 0)
-            grouped = keep.tile([P, hi - lo, PACK], BF16, name=f"w_grouped{e}_{a}_{lo}", align_bytes=64)
-            interleave(nc, engine, grouped[:], w_raw[e, a, src][:, :, lo - src:hi - src])
-            return grouped
+        def gather(target, table, h):
+            nc.vector.tensor_copy(out=target[:, h * HALF:(h + 1) * HALF], in_=table[:].indirect(offs_sb[:, h * 16:(h + 1) * 16]))
 
-        W_ENGINE = {(0, 0, 0): "scalar", (0, 0, 256): "vector", (0, 1, 0): "scalar", (0, 1, 256): "vector",
-                    (3, 0, 256): "vector"}
+        def take_w(e, a):
+            for lo, hi in ((0, 256), (256, 384)):
+                grouped = keep.tile([P, hi - lo, PACK], BF16, name=f"w_grouped{e}_{a}_{lo}", align_bytes=64)
+                engine = "vector" if (a == 1 and e < 3 and lo == 256) else ("gpsimd" if False else "scalar")
+                interleave(nc, engine, grouped[:], w_raw[e, a][:, :, lo:hi])
+                quantize(nc, w_codes[e, a][:, lo:hi], w_scales[e, a][:, lo:hi], grouped[:])
+
         products = {}
-        w_codes, w_scales = {}, {}
-        for e in range(E):
-            for a in range(PASSES):
-                w_codes[e, a] = keep.tile([P, N], U32, name=f"w_codes{e}_{a}", align_bytes=64)
-                w_scales[e, a] = keep.tile([P, N], U8, name=f"w_scales{e}_{a}", align_bytes=64)
 
-        def multiply(e, n, acc):
-            cols = slice(n * P, (n + 1) * P)
+        def multiply(e):
             slots = slice(e * C, (e + 1) * C)
-            for a in range(PASSES):
-                nc.tensor.matmul_mx(
-                    out=acc[:],
-                    lhsT=w_codes[e, a][:, cols].bitcast(FP8X4),
-                    lhsT_scale=w_scales[e, a][:, cols],
-                    rhs=slot_codes[a][:, slots].bitcast(FP8X4),
-                    rhs_scale=slot_scales[4 * a:P, slots],
-                    start=(a == 0), stop=(a == PASSES - 1))
-
-        def finish(e, n, acc):
-            y = keep.tile([P, C], F32, name=f"y{e}_{n}")
-            nc.vector.scalar_tensor_tensor(y[:], acc[:], b_sb[:, n, e:e + 1], gate_sb[:, n, e * C:(e + 1) * C], ADD, MULT)
-            products[e, n] = y
+            for n in range(N_TILES):
+                cols = slice(n * P, (n + 1) * P)
+                acc = psum.tile([P, C], F32, name="acc")
+                for a in range(PASSES):
+                    nc.tensor.matmul_mx(
+                        out=acc[:],
+                        lhsT=w_codes[e, a][:, cols].bitcast(FP8X4),
+                        lhsT_scale=w_scales[e, a][:, cols],
+                        rhs=slot_codes[a][:, slots].bitcast(FP8X4),
+                        rhs_scale=slot_scales[4 * a:P, slots],
+                        start=(a == 0), stop=(a == PASSES - 1))
+                products[e, n] = acc
+            for n in range(N_TILES):
+                y = keep.tile([P, C], F32, name=f"y{e}_{n}")
+                nc.scalar.activation(y[:], products[e, n][:], IDENTITY, bias=b_sb[:, n, e:e + 1])
+                products[e, n] = y
 
         def scatter(e, n):
-            nc.vector.tensor_copy(
-                out=windows[n][:].indirect(dst_sb[:, e * 8:(e + 1) * 8]),
-                in_=products[e, n][:])
+            window = windows[n][:].indirect(dst_sb[:, e * 8:(e + 1) * 8])
+            nc.vector.tensor_tensor(window, products[e, n][:], gate_sb[:, n, e * C:(e + 1) * C], MULT)
 
-        for e in range(E):
-            order = [(0, 0, 256), (0, 256, N), (1, 0, 256), (1, 256, N)]
-            if e == E - 1:
-                order = [(0, 0, 256), (1, 0, 256), (0, 256, N), (1, 256, N)]
-            for a, lo, hi in order:
-                grouped = take_w(e, a, lo, hi, W_ENGINE.get((e, a, lo), "scalar"))
-                quantize(nc, w_codes[e, a][:, lo:hi], w_scales[e, a][:, lo:hi], grouped[:])
-            accs = []
+        take_x(0)
+        gather(slot_codes[0], x_codes[0], 0)
+        take_x(1)
+        gather(slot_codes[1], x_codes[1], 0)
+        gather(slot_scales, x_scales, 0)
+        take_w(0, 0)
+        take_w(0, 1)
+        multiply(0)
+        gather(slot_codes[0], x_codes[0], 1)
+        gather(slot_codes[1], x_codes[1], 1)
+        gather(slot_scales, x_scales, 1)
+        for e in range(1, E):
+            for a in range(PASSES):
+                take_w(e, a)
+            multiply(e)
             for n in range(N_TILES):
-                acc = psum.tile([P, C], F32, name="acc")
-                multiply(e, n, acc)
-                accs.append(acc)
-            for n in range(N_TILES):
-                finish(e, n, accs[n])
-            if e > 0:
-                for n in range(N_TILES):
-                    scatter(e - 1, n)
+                scatter(e - 1, n)
         for n in range(N_TILES):
             scatter(E - 1, n)
             nc.sync.dma_start(out=out[n * P:(n + 1) * P, :], in_=windows[n][:])

@@ -8,6 +8,7 @@ FLOPS = 2 * K * N * E * C
 F32 = mybir.dt.float32
 BF16 = mybir.dt.bfloat16
 U32 = mybir.dt.uint32
+I32 = mybir.dt.int32
 U16 = mybir.dt.uint16
 U8 = mybir.dt.uint8
 FP8X4 = mybir.dt.float8_e4m3fn_x4
@@ -22,7 +23,8 @@ K_PASS = P * PACK
 PASSES = K // K_PASS
 N_TILES = N // P
 SLOTS = E * C
-HALF = SLOTS // 2
+T_PAD = 704
+CUT = 256
 
 
 def interleave(nc, engine, grouped, raw):
@@ -56,103 +58,182 @@ def tile_moe_two_lin_bias_kernel(tc, xT, w, b, gate, offs, dst, out):
         gate_sb = keep.tile([P, N_TILES, SLOTS], F32, name="gate_sb")
         warm = keep.tile([P, 8], F32, name="warm")
         windows = [keep.tile([P, T], F32, name=f"window{n}") for n in range(N_TILES)]
-        x_scales = keep.tile([P, T], U8, name="x_scales", align_bytes=64)
+        x_scales = keep.tile([P, T_PAD], U8, name="x_scales", align_bytes=64)
         slot_scales = keep.tile([P, SLOTS], U8, name="slot_scales", align_bytes=64)
-        x_codes = [keep.tile([P, T], U32, name=f"x_codes{a}", align_bytes=64) for a in range(PASSES)]
+        x_codes = [keep.tile([P, T_PAD], U32, name=f"x_codes{a}", align_bytes=64) for a in range(PASSES)]
         slot_codes = [keep.tile([P, SLOTS], U32, name=f"slot_codes{a}", align_bytes=64) for a in range(PASSES)]
         x_raw = [keep.tile([P, PACK, T], F32, name=f"x_raw{a}") for a in range(PASSES)]
-        w_raw = {(e, a): keep.tile([P, PACK, N], F32, name=f"w_raw{e}_{a}") for e in range(E) for a in range(PASSES)}
-        w_codes = {(e, a): keep.tile([P, N], U32, name=f"w_codes{e}_{a}", align_bytes=64) for e in range(E) for a in range(PASSES)}
-        w_scales = {(e, a): keep.tile([P, N], U8, name=f"w_scales{e}_{a}", align_bytes=64) for e in range(E) for a in range(PASSES)}
 
         nc.vector.memset(warm[:], 0.0)
         nc.scalar.activation(warm[:, 1:2], warm[:, 0:1], IDENTITY)
         nc.gpsimd.memset(x_scales[:], 0)
+        for codes in x_codes:
+            nc.gpsimd.memset(codes[:, T:T_PAD].bitcast(I32), 0)
         for window in windows:
             nc.vector.memset(window[:], 0.0)
 
         nc.scalar.dma_start(out=b_sb[:, :, 0:E], in_=b.rearrange("(t p) e -> p t e", p=P))
 
-        def load_x(a):
-            nc.sync.dma_start(out=x_raw[a][:], in_=xT[a * K_PASS:(a + 1) * K_PASS, :].rearrange("(p j) t -> p j t", j=PACK))
+        w_raw, w_codes, w_scales, w_grouped = {}, {}, {}, {}
+        CUTS = ((0, CUT), (CUT, N))
+        for e in range(E):
+            for lo, hi in CUTS:
+                w_grouped[e, lo] = keep.tile([P, PASSES, hi - lo, PACK], BF16, name=f"w_grouped{e}_{lo}", align_bytes=64)
+                w_codes[e, lo] = keep.tile([P, PASSES, hi - lo], U32, name=f"w_codes{e}_{lo}", align_bytes=64)
+                w_scales[e, lo] = keep.tile([P, PASSES, hi - lo], U8, name=f"w_scales{e}_{lo}", align_bytes=64)
+        x_grouped = [keep.tile([P, T, PACK], BF16, name=f"x_grouped{a}", align_bytes=64) for a in range(PASSES)]
 
-        def load_w(e, a):
-            nc.sync.dma_start(out=w_raw[e, a][:], in_=w[e, a * K_PASS:(a + 1) * K_PASS, :].rearrange("(p j) n -> p j n", j=PACK))
+        def load(kind, *s):
+            if kind == "x":
+                a, lo, hi = s
+                nc.sync.dma_start(out=x_raw[a][:, :, lo:hi], in_=xT[a * K_PASS:(a + 1) * K_PASS, lo:hi].rearrange("(p j) t -> p j t", j=PACK))
+            elif kind == "w":
+                e, a, lo, hi = s
+                raw = keep.tile([P, PACK, hi - lo], F32, name=f"w_raw{e}_{a}_{lo}")
+                nc.sync.dma_start(out=raw[:], in_=w[e, a * K_PASS:(a + 1) * K_PASS, lo:hi].rearrange("(p j) n -> p j n", j=PACK))
+                for c0, c1 in CUTS:
+                    if lo <= c0 and c1 <= hi:
+                        w_raw[e, a, c0] = (raw, c0 - lo, c1 - lo)
+            elif kind == "gate":
+                nc.sync.dma_start(out=gate_sb[:], in_=gate.rearrange("(t p) s -> p t s", p=P))
+            elif kind == "offs":
+                nc.sync.dma_start(offs_sb[:], offs)
+            else:
+                nc.sync.dma_start(dst_sb[:], dst)
 
-        load_x(0)
-        nc.sync.dma_start(offs_sb[:], offs)
-        load_x(1)
-        nc.sync.dma_start(dst_sb[:], dst)
-        load_w(0, 0)
-        load_w(0, 1)
-        nc.sync.dma_start(out=gate_sb[:], in_=gate.rearrange("(t p) s -> p t s", p=P))
-        for e in range(1, E):
-            for a in range(PASSES):
-                load_w(e, a)
+        for s in [("x", 0, 0, 256), ("x", 0, 256, 640), ("offs",), ("w", 0, 0, 0, 384), ("x", 1, 0, 256), ("x", 1, 256, 640), ("dst",), ("w", 0, 1, 0, 384), ("w", 1, 0, 0, 384), ("gate",), ("w", 1, 1, 0, 384), ("w", 2, 0, 0, 384), ("w", 2, 1, 0, 384), ("w", 3, 0, 0, 256), ("w", 3, 1, 0, 256), ("w", 3, 0, 256, 384), ("w", 3, 1, 256, 384)]:
+            load(*s)
 
-        X_ENGINES = (("scalar", "vector", "vector"), ("scalar", "vector", "scalar"))
-
-        def take_x(a):
-            pieces = []
-            for (lo, hi), engine in zip(((0, 256), (256, 512), (512, 640)), X_ENGINES[a]):
-                grouped = keep.tile([P, hi - lo, PACK], BF16, name=f"x_grouped{a}_{lo}", align_bytes=64)
-                interleave(nc, engine, grouped[:], x_raw[a][:, :, lo:hi])
-                pieces.append((lo, hi, grouped))
-            for lo, hi, grouped in pieces:
-                quantize(nc, x_codes[a][:, lo:hi], x_scales[4 * a:P, lo:hi], grouped[:])
-
-        def gather(target, table, h):
-            nc.vector.tensor_copy(out=target[:, h * HALF:(h + 1) * HALF], in_=table[:].indirect(offs_sb[:, h * 16:(h + 1) * 16]))
-
-        def take_w(e, a):
-            for lo, hi in ((0, 256), (256, 384)):
-                grouped = keep.tile([P, hi - lo, PACK], BF16, name=f"w_grouped{e}_{a}_{lo}", align_bytes=64)
-                engine = "vector" if (a == 1 and e < 3 and lo == 256) else ("gpsimd" if False else "scalar")
-                interleave(nc, engine, grouped[:], w_raw[e, a][:, :, lo:hi])
-                quantize(nc, w_codes[e, a][:, lo:hi], w_scales[e, a][:, lo:hi], grouped[:])
-
-        products = {}
-
-        def multiply(e):
-            slots = slice(e * C, (e + 1) * C)
-            for n in range(N_TILES):
-                cols = slice(n * P, (n + 1) * P)
+        accs, ys = {}, {}
+        left = [E] * N_TILES
+        STEPS = [
+            ("ix", 0, 0, 256, "vector"),
+            ("ix", 0, 256, 512, "scalar"),
+            ("ix", 0, 512, 640, "vector"),
+            ("qx", 0, 0, 256),
+            ("qx", 0, 256, 512),
+            ("qx", 0, 512, 640),
+            ("gw", 0, 0),
+            ("gw", 0, 1),
+            ("iw", 0, 0, 0, 256, "scalar"),
+            ("iw", 0, 0, 256, 384, "scalar"),
+            ("ix", 1, 0, 256, "scalar"),
+            ("ix", 1, 256, 512, "vector"),
+            ("ix", 1, 512, 640, "scalar"),
+            ("qx", 1, 0, 256),
+            ("qx", 1, 256, 512),
+            ("qx", 1, 512, 640),
+            ("gw", 1, 0),
+            ("gb", 0),
+            ("gw", 1, 1),
+            ("gb", 1),
+            ("iw", 0, 1, 0, 256, "scalar"),
+            ("iw", 0, 1, 256, 384, "scalar"),
+            ("qw", 0, 0, 1, 0, 256),
+            ("qw", 0, 0, 1, 256, 384),
+            ("qw", 0, 1, 2, 0, 256),
+            ("qw", 0, 1, 2, 256, 384),
+            ("iw", 1, 0, 0, 256, "scalar"),
+            ("iw", 1, 0, 256, 384, "scalar"),
+            ("mm", 0, 0),
+            ("mm", 0, 1),
+            ("mm", 0, 2),
+            ("ev", 0, 0),
+            ("ev", 0, 1),
+            ("ev", 0, 2),
+            ("iw", 1, 1, 0, 256, "scalar"),
+            ("iw", 1, 1, 256, 384, "scalar"),
+            ("qw", 1, 0, 2, 0, 256),
+            ("qw", 1, 0, 2, 256, 384),
+            ("sc", 0, 0),
+            ("sc", 0, 1),
+            ("sc", 0, 2),
+            ("iw", 2, 0, 0, 256, "scalar"),
+            ("iw", 2, 0, 256, 384, "scalar"),
+            ("mm", 1, 0),
+            ("mm", 1, 1),
+            ("mm", 1, 2),
+            ("ev", 1, 0),
+            ("ev", 1, 1),
+            ("ev", 1, 2),
+            ("iw", 2, 1, 0, 256, "scalar"),
+            ("iw", 2, 1, 256, 384, "scalar"),
+            ("qw", 2, 0, 2, 0, 256),
+            ("qw", 2, 0, 2, 256, 384),
+            ("sc", 1, 0),
+            ("sc", 1, 1),
+            ("sc", 1, 2),
+            ("iw", 3, 0, 0, 256, "scalar"),
+            ("iw", 3, 1, 0, 256, "scalar"),
+            ("mm", 2, 0),
+            ("mm", 2, 1),
+            ("mm", 2, 2),
+            ("ev", 2, 0),
+            ("ev", 2, 1),
+            ("ev", 2, 2),
+            ("iw", 3, 0, 256, 384, "scalar"),
+            ("iw", 3, 1, 256, 384, "scalar"),
+            ("qw", 3, 0, 2, 0, 256),
+            ("qw", 3, 0, 2, 256, 384),
+            ("sc", 2, 0),
+            ("sc", 2, 1),
+            ("sc", 2, 2),
+            ("mm", 3, 0),
+            ("mm", 3, 1),
+            ("mm", 3, 2),
+            ("ev", 3, 0),
+            ("ev", 3, 1),
+            ("ev", 3, 2),
+            ("sc", 3, 0),
+            ("sc", 3, 1),
+            ("sc", 3, 2),
+        ]
+        for step in STEPS:
+            kind, s = step[0], step[1:]
+            if kind == "ix":
+                a, lo, hi, engine = s
+                interleave(nc, engine, x_grouped[a][:, lo:hi, :], x_raw[a][:, :, lo:hi])
+            elif kind == "qx":
+                a, lo, hi = s
+                quantize(nc, x_codes[a][:, lo:hi], x_scales[4 * a:P, lo:hi], x_grouped[a][:, lo:hi, :])
+            elif kind in ("gw", "gb"):
+                target, table = (slot_codes[s[0]], x_codes[s[0]]) if kind == "gw" else (slot_scales, x_scales)
+                h = s[1:] if kind == "gw" else s
+                if h:
+                    nc.vector.tensor_copy(out=target[:, h[0] * 256:(h[0] + 1) * 256], in_=table[:].indirect(offs_sb[:, h[0] * 16:(h[0] + 1) * 16]))
+                else:
+                    nc.vector.tensor_copy(out=target[:], in_=table[:].indirect(offs_sb[:]))
+            elif kind == "iw":
+                e, a, lo, hi, engine = s
+                raw, c0, c1 = w_raw[e, a, lo]
+                interleave(nc, engine, w_grouped[e, lo][:, a, :, :], raw[:, :, c0:c1])
+            elif kind == "qw":
+                e, a0, a1, lo, hi = s
+                nc.vector.quantize_mx(
+                    out=w_codes[e, lo][:, a0:a1, :].rearrange("p a n -> p (a n)").bitcast(FP8X4),
+                    scales=w_scales[e, lo][:, a0:a1, :].rearrange("p a n -> p (a n)"),
+                    in_=w_grouped[e, lo][:, a0:a1, :, :].rearrange("p a n j -> p (a n j)"))
+            elif kind == "mm":
+                e, n = s
                 acc = psum.tile([P, C], F32, name="acc")
+                accs[e, n] = acc
+                lo = 0 if n < 2 else CUT
                 for a in range(PASSES):
                     nc.tensor.matmul_mx(
                         out=acc[:],
-                        lhsT=w_codes[e, a][:, cols].bitcast(FP8X4),
-                        lhsT_scale=w_scales[e, a][:, cols],
-                        rhs=slot_codes[a][:, slots].bitcast(FP8X4),
-                        rhs_scale=slot_scales[4 * a:P, slots],
+                        lhsT=w_codes[e, lo][:, a, n * P - lo:(n + 1) * P - lo].bitcast(FP8X4),
+                        lhsT_scale=w_scales[e, lo][:, a, n * P - lo:(n + 1) * P - lo],
+                        rhs=slot_codes[a][:, e * C:(e + 1) * C].bitcast(FP8X4),
+                        rhs_scale=slot_scales[4 * a:P, e * C:(e + 1) * C],
                         start=(a == 0), stop=(a == PASSES - 1))
-                products[e, n] = acc
-            for n in range(N_TILES):
+            elif kind == "ev":
+                e, n = s
                 y = keep.tile([P, C], F32, name=f"y{e}_{n}")
-                nc.scalar.activation(y[:], products[e, n][:], IDENTITY, bias=b_sb[:, n, e:e + 1])
-                products[e, n] = y
-
-        def scatter(e, n):
-            window = windows[n][:].indirect(dst_sb[:, e * 8:(e + 1) * 8])
-            nc.vector.tensor_tensor(window, products[e, n][:], gate_sb[:, n, e * C:(e + 1) * C], MULT)
-
-        take_x(0)
-        gather(slot_codes[0], x_codes[0], 0)
-        take_x(1)
-        gather(slot_codes[1], x_codes[1], 0)
-        gather(slot_scales, x_scales, 0)
-        take_w(0, 0)
-        take_w(0, 1)
-        multiply(0)
-        gather(slot_codes[0], x_codes[0], 1)
-        gather(slot_codes[1], x_codes[1], 1)
-        gather(slot_scales, x_scales, 1)
-        for e in range(1, E):
-            for a in range(PASSES):
-                take_w(e, a)
-            multiply(e)
-            for n in range(N_TILES):
-                scatter(e - 1, n)
-        for n in range(N_TILES):
-            scatter(E - 1, n)
-            nc.sync.dma_start(out=out[n * P:(n + 1) * P, :], in_=windows[n][:])
+                ys[e, n] = y
+                nc.scalar.activation(y[:], accs[e, n][:], IDENTITY, bias=b_sb[:, n, e:e + 1])
+            else:
+                e, n = s
+                nc.vector.tensor_tensor(windows[n][:].indirect(dst_sb[:, e * 8:(e + 1) * 8]), ys[e, n][:], gate_sb[:, n, e * C:(e + 1) * C], MULT)
+                left[n] -= 1
+                if left[n] == 0:
+                    nc.sync.dma_start(out=out[n * P:(n + 1) * P, :], in_=windows[n][:])

from contextlib import ExitStack

import concourse.mybir as mybir

K, T, E, C, N = 1024, 640, 4, 128, 384
FLOPS = 2 * K * N * E * C

F32 = mybir.dt.float32
BF16 = mybir.dt.bfloat16
U32 = mybir.dt.uint32
I32 = mybir.dt.int32
U16 = mybir.dt.uint16
U8 = mybir.dt.uint8
FP8X4 = mybir.dt.float8_e4m3fn_x4
COPY = mybir.ActivationFunctionType.Copy
IDENTITY = mybir.ActivationFunctionType.Identity
MULT = mybir.AluOpType.mult
ADD = mybir.AluOpType.add

P = 128
PACK = 4
K_PASS = P * PACK
PASSES = K // K_PASS
N_TILES = N // P
SLOTS = E * C
T_PAD = 704
CUT = 256


def interleave(nc, engine, grouped, raw):
    dst = grouped.rearrange("p (c i) j -> p c j i", i=4)
    src = raw.rearrange("p j (c i) -> p c j i", i=4)
    if engine == "vector":
        nc.vector.tensor_copy(out=dst, in_=src)
    elif engine == "gpsimd":
        nc.gpsimd.tensor_scalar(dst, src, 1.0, 0.0, MULT, ADD)
    else:
        nc.scalar.activation(dst, src, COPY)


def quantize(nc, codes, scales, grouped):
    nc.vector.quantize_mx(
        out=codes.bitcast(FP8X4),
        scales=scales,
        in_=grouped.rearrange("p w j -> p (w j)"),
    )


def tile_moe_two_lin_bias_kernel(tc, xT, w, b, gate, offs, dst, out):
    nc = tc.nc
    with ExitStack() as ctx:
        keep = ctx.enter_context(tc.tile_pool(name="keep", bufs=1))
        psum = ctx.enter_context(tc.psum_pool(name="psum", bufs=8))

        offs_sb = keep.tile([P, SLOTS // 16], U16, name="offs_sb")
        dst_sb = keep.tile([P, SLOTS // 16], U16, name="dst_sb")
        b_sb = keep.tile([P, N_TILES, 8], F32, name="b_sb")
        gate_sb = keep.tile([P, N_TILES, SLOTS], F32, name="gate_sb")
        warm = keep.tile([P, 8], F32, name="warm")
        windows = [keep.tile([P, T], F32, name=f"window{n}") for n in range(N_TILES)]
        x_scales = keep.tile([P, T_PAD], U8, name="x_scales", align_bytes=64)
        slot_scales = keep.tile([P, SLOTS], U8, name="slot_scales", align_bytes=64)
        x_codes = [keep.tile([P, T_PAD], U32, name=f"x_codes{a}", align_bytes=64) for a in range(PASSES)]
        slot_codes = [keep.tile([P, SLOTS], U32, name=f"slot_codes{a}", align_bytes=64) for a in range(PASSES)]
        x_raw = [keep.tile([P, PACK, T], F32, name=f"x_raw{a}") for a in range(PASSES)]

        nc.vector.memset(warm[:], 0.0)
        nc.scalar.activation(warm[:, 1:2], warm[:, 0:1], IDENTITY)
        nc.gpsimd.memset(x_scales[:], 0)
        for codes in x_codes:
            nc.gpsimd.memset(codes[:, T:T_PAD].bitcast(I32), 0)
        for window in windows:
            nc.vector.memset(window[:], 0.0)

        nc.scalar.dma_start(out=b_sb[:, :, 0:E], in_=b.rearrange("(t p) e -> p t e", p=P))

        w_raw, w_codes, w_scales, w_grouped = {}, {}, {}, {}
        CUTS = ((0, CUT), (CUT, N))
        for e in range(E):
            for lo, hi in CUTS:
                w_grouped[e, lo] = keep.tile([P, PASSES, hi - lo, PACK], BF16, name=f"w_grouped{e}_{lo}", align_bytes=64)
                w_codes[e, lo] = keep.tile([P, PASSES, hi - lo], U32, name=f"w_codes{e}_{lo}", align_bytes=64)
                w_scales[e, lo] = keep.tile([P, PASSES, hi - lo], U8, name=f"w_scales{e}_{lo}", align_bytes=64)
        x_grouped = [keep.tile([P, T, PACK], BF16, name=f"x_grouped{a}", align_bytes=64) for a in range(PASSES)]

        def load(kind, *s):
            if kind == "x":
                a, lo, hi = s
                nc.sync.dma_start(out=x_raw[a][:, :, lo:hi], in_=xT[a * K_PASS:(a + 1) * K_PASS, lo:hi].rearrange("(p j) t -> p j t", j=PACK))
            elif kind == "w":
                e, a, lo, hi = s
                raw = keep.tile([P, PACK, hi - lo], F32, name=f"w_raw{e}_{a}_{lo}")
                nc.sync.dma_start(out=raw[:], in_=w[e, a * K_PASS:(a + 1) * K_PASS, lo:hi].rearrange("(p j) n -> p j n", j=PACK))
                for c0, c1 in CUTS:
                    if lo <= c0 and c1 <= hi:
                        w_raw[e, a, c0] = (raw, c0 - lo, c1 - lo)
            elif kind == "gate":
                nc.sync.dma_start(out=gate_sb[:], in_=gate.rearrange("(t p) s -> p t s", p=P))
            elif kind == "offs":
                nc.sync.dma_start(offs_sb[:], offs)
            else:
                nc.sync.dma_start(dst_sb[:], dst)

        for s in [("x", 0, 0, 256), ("x", 0, 256, 640), ("offs",), ("w", 0, 0, 0, 384), ("x", 1, 0, 256), ("x", 1, 256, 640), ("dst",), ("w", 0, 1, 0, 384), ("w", 1, 0, 0, 384), ("gate",), ("w", 1, 1, 0, 384), ("w", 2, 0, 0, 384), ("w", 2, 1, 0, 384), ("w", 3, 0, 0, 256), ("w", 3, 1, 0, 256), ("w", 3, 0, 256, 384), ("w", 3, 1, 256, 384)]:
            load(*s)

        accs, ys = {}, {}
        left = [E] * N_TILES
        STEPS = [
            ("ix", 0, 0, 256, "vector"),
            ("ix", 0, 256, 512, "scalar"),
            ("ix", 0, 512, 640, "vector"),
            ("qx", 0, 0, 256),
            ("qx", 0, 256, 512),
            ("qx", 0, 512, 640),
            ("gw", 0, 0),
            ("gw", 0, 1),
            ("iw", 0, 0, 0, 256, "scalar"),
            ("iw", 0, 0, 256, 384, "scalar"),
            ("ix", 1, 0, 256, "scalar"),
            ("ix", 1, 256, 512, "vector"),
            ("ix", 1, 512, 640, "scalar"),
            ("qx", 1, 0, 256),
            ("qx", 1, 256, 512),
            ("qx", 1, 512, 640),
            ("gw", 1, 0),
            ("gb", 0),
            ("gw", 1, 1),
            ("gb", 1),
            ("iw", 0, 1, 0, 256, "scalar"),
            ("iw", 0, 1, 256, 384, "scalar"),
            ("qw", 0, 0, 1, 0, 256),
            ("qw", 0, 0, 1, 256, 384),
            ("qw", 0, 1, 2, 0, 256),
            ("qw", 0, 1, 2, 256, 384),
            ("iw", 1, 0, 0, 256, "scalar"),
            ("iw", 1, 0, 256, 384, "scalar"),
            ("mm", 0, 0),
            ("mm", 0, 1),
            ("mm", 0, 2),
            ("ev", 0, 0),
            ("ev", 0, 1),
            ("ev", 0, 2),
            ("iw", 1, 1, 0, 256, "scalar"),
            ("iw", 1, 1, 256, 384, "scalar"),
            ("qw", 1, 0, 2, 0, 256),
            ("qw", 1, 0, 2, 256, 384),
            ("sc", 0, 0),
            ("sc", 0, 1),
            ("sc", 0, 2),
            ("iw", 2, 0, 0, 256, "scalar"),
            ("iw", 2, 0, 256, 384, "scalar"),
            ("mm", 1, 0),
            ("mm", 1, 1),
            ("mm", 1, 2),
            ("ev", 1, 0),
            ("ev", 1, 1),
            ("ev", 1, 2),
            ("iw", 2, 1, 0, 256, "scalar"),
            ("iw", 2, 1, 256, 384, "scalar"),
            ("qw", 2, 0, 2, 0, 256),
            ("qw", 2, 0, 2, 256, 384),
            ("sc", 1, 0),
            ("sc", 1, 1),
            ("sc", 1, 2),
            ("iw", 3, 0, 0, 256, "scalar"),
            ("iw", 3, 1, 0, 256, "scalar"),
            ("mm", 2, 0),
            ("mm", 2, 1),
            ("mm", 2, 2),
            ("ev", 2, 0),
            ("ev", 2, 1),
            ("ev", 2, 2),
            ("iw", 3, 0, 256, 384, "scalar"),
            ("iw", 3, 1, 256, 384, "scalar"),
            ("qw", 3, 0, 2, 0, 256),
            ("qw", 3, 0, 2, 256, 384),
            ("sc", 2, 0),
            ("sc", 2, 1),
            ("sc", 2, 2),
            ("mm", 3, 0),
            ("mm", 3, 1),
            ("mm", 3, 2),
            ("ev", 3, 0),
            ("ev", 3, 1),
            ("ev", 3, 2),
            ("sc", 3, 0),
            ("sc", 3, 1),
            ("sc", 3, 2),
        ]
        for step in STEPS:
            kind, s = step[0], step[1:]
            if kind == "ix":
                a, lo, hi, engine = s
                interleave(nc, engine, x_grouped[a][:, lo:hi, :], x_raw[a][:, :, lo:hi])
            elif kind == "qx":
                a, lo, hi = s
                quantize(nc, x_codes[a][:, lo:hi], x_scales[4 * a:P, lo:hi], x_grouped[a][:, lo:hi, :])
            elif kind in ("gw", "gb"):
                target, table = (slot_codes[s[0]], x_codes[s[0]]) if kind == "gw" else (slot_scales, x_scales)
                h = s[1:] if kind == "gw" else s
                if h:
                    nc.vector.tensor_copy(out=target[:, h[0] * 256:(h[0] + 1) * 256], in_=table[:].indirect(offs_sb[:, h[0] * 16:(h[0] + 1) * 16]))
                else:
                    nc.vector.tensor_copy(out=target[:], in_=table[:].indirect(offs_sb[:]))
            elif kind == "iw":
                e, a, lo, hi, engine = s
                raw, c0, c1 = w_raw[e, a, lo]
                interleave(nc, engine, w_grouped[e, lo][:, a, :, :], raw[:, :, c0:c1])
            elif kind == "qw":
                e, a0, a1, lo, hi = s
                nc.vector.quantize_mx(
                    out=w_codes[e, lo][:, a0:a1, :].rearrange("p a n -> p (a n)").bitcast(FP8X4),
                    scales=w_scales[e, lo][:, a0:a1, :].rearrange("p a n -> p (a n)"),
                    in_=w_grouped[e, lo][:, a0:a1, :, :].rearrange("p a n j -> p (a n j)"))
            elif kind == "mm":
                e, n = s
                acc = psum.tile([P, C], F32, name="acc")
                accs[e, n] = acc
                lo = 0 if n < 2 else CUT
                for a in range(PASSES):
                    nc.tensor.matmul_mx(
                        out=acc[:],
                        lhsT=w_codes[e, lo][:, a, n * P - lo:(n + 1) * P - lo].bitcast(FP8X4),
                        lhsT_scale=w_scales[e, lo][:, a, n * P - lo:(n + 1) * P - lo],
                        rhs=slot_codes[a][:, e * C:(e + 1) * C].bitcast(FP8X4),
                        rhs_scale=slot_scales[4 * a:P, e * C:(e + 1) * C],
                        start=(a == 0), stop=(a == PASSES - 1))
            elif kind == "ev":
                e, n = s
                y = keep.tile([P, C], F32, name=f"y{e}_{n}")
                ys[e, n] = y
                nc.scalar.activation(y[:], accs[e, n][:], IDENTITY, bias=b_sb[:, n, e:e + 1])
            else:
                e, n = s
                nc.vector.tensor_tensor(windows[n][:].indirect(dst_sb[:, e * 8:(e + 1) * 8]), ys[e, n][:], gate_sb[:, n, e * C:(e + 1) * C], MULT)
                left[n] -= 1
                if left[n] == 0:
                    nc.sync.dma_start(out=out[n * P:(n + 1) * P, :], in_=windows[n][:])
